import numpy as np
import ml_dtypes


def mxq(x, axis, fmt="e4m3"):
    dtype, down = {"e4m3": (ml_dtypes.float8_e4m3fn, 7), "e5m2": (ml_dtypes.float8_e5m2, 14)}[fmt]
    v = np.moveaxis(np.asarray(x, np.float32).astype(ml_dtypes.bfloat16).astype(np.float64), axis, -1)
    blocks = v.reshape(v.shape[:-1] + (-1, 32))
    amax = np.abs(blocks).max(-1, keepdims=True)
    byte = np.maximum(np.where(amax > 0, np.frexp(amax)[1] - 1 + 127, 0) - down, 1)
    scale = np.exp2(byte - 127.0)
    codes = (blocks / scale).astype(np.float32).astype(dtype).astype(np.float64)
    return np.moveaxis((codes * scale).reshape(v.shape), -1, axis)


WIDE = False


def mx_kscale(k):
    if not WIDE:
        return np.ones(k)
    levels = np.array([10, -10, 5, -5, 0])
    if k % 512:
        return np.exp2(np.random.permutation(np.resize(levels, k // 32))).repeat(32)
    a = np.empty((k // 512, 16))
    for p in range(k // 512):
        a[p, :8] = np.random.permutation(np.resize(levels, 8))
        for g in range(8):
            far = levels[np.abs(levels - a[p, g]) >= 10]
            a[p, g + 8] = far[np.random.randint(len(far))]
    return np.exp2(a.ravel()).repeat(32)


def f64(x):
    return np.asarray(x).astype(np.float64)


def striped8(idx):
    return np.asarray(idx).reshape(8, -1, 16).transpose(0, 2, 1).reshape(128, -1).astype(np.uint16)


def unstriped8(offs):
    return offs.reshape(8, 16, -1).transpose(0, 2, 1).reshape(8, -1).astype(np.int64)


def pick8(x, idx, run):
    r = np.arange(len(x))
    return x[r[:, None], idx[r % (8 * run) // run]]


E2M1 = np.array([0.0, 0.5, 1.0, 1.5, 2.0, 3.0, 4.0, 6.0, -0.0, -0.5, -1.0, -1.5, -2.0, -3.0, -4.0, -6.0])


def pack_weight(w, fmt):
    k, n = w.shape
    w = f64(np.asarray(w, np.float32).astype(ml_dtypes.bfloat16)).reshape(k // 32, 32, n)
    amax = np.abs(w).max(1)
    if fmt == "e4m3":
        byte = np.frexp(amax)[1] - 1 + 127 - 7
    else:
        mant, ex = np.frexp(amax / 6.0)
        byte = np.where(mant > 0.5, ex, ex - 1) + 127
    byte = np.clip(np.where(amax > 0, byte, 1), 1, 254)
    scaled = (w * np.exp2(127.0 - byte)[:, None, :]).reshape(k, n).astype(np.float32)
    by_word = np.ascontiguousarray(scaled.reshape(k // 512, 128, 4, n).transpose(0, 1, 3, 2))
    if fmt == "e4m3":
        words = by_word.astype(ml_dtypes.float8_e4m3fn).view(np.uint8)
    else:
        c = by_word.astype(ml_dtypes.float4_e2m1fn).view(np.uint8) & 0xF
        words = (c[..., 0::2] | (c[..., 1::2] << 4)).reshape(k // 512, 128, 2 * n)
    return np.ascontiguousarray(words), np.ascontiguousarray(byte.astype(np.uint8).reshape(k // 512, 16, n))


def unpack_weight(words, scales, fmt):
    g, _, n = scales.shape
    words = np.ascontiguousarray(words).reshape(g, 128, n, -1)
    if fmt == "e4m3":
        vals = words.view(ml_dtypes.float8_e4m3fn).astype(np.float64)
    else:
        nib = np.empty((g, 128, n, 4), np.uint8)
        nib[..., 0::2] = words & 0xF
        nib[..., 1::2] = words >> 4
        vals = E2M1[nib]
    vals = vals * np.repeat(np.exp2(scales.astype(np.float64) - 127.0), 8, axis=1)[..., None]
    return vals.transpose(0, 1, 3, 2).reshape(g * 512, n)


D, T, I, Q = 512, 1024, 512, 128


def setup_inputs():
    n = np.random.standard_normal
    idx = np.stack([np.random.permutation(T)[:I] for _ in range(8)])
    idx2 = np.stack([np.random.permutation(T)[:I] for _ in range(8)])
    idx3 = np.stack([np.random.permutation(T)[:I] for _ in range(8)])
    fd = mx_kscale(D)
    keysp = pack_weight(n((D, T)) / fd[:, None], "e2m1")
    return {
        "query": (n((D, Q)) * 0.9 / np.sqrt(D) * fd[:, None]).astype(np.float32),
        "query2": (n((D, Q)) * 0.9 / np.sqrt(D) * fd[:, None]).astype(np.float32),
        "keys_words": keysp[0],
        "keys_scales": keysp[1],
        "lam": (np.random.uniform(1.0, 2.5, (Q, 1))).astype(np.float32),
        "pull": (np.random.uniform(0.3, 0.9, (Q, 1))).astype(np.float32),
        "old": (np.random.uniform(0.0, 2.0, (Q, T))).astype(np.float32),
        "fade": (np.random.uniform(0.3, 0.9, (Q, 1))).astype(np.float32),
        "offs": striped8(idx),
        "offs2": striped8(idx2),
        "offs3": striped8(idx3),
    }


def reference(query, query2, keys_words, keys_scales, lam, pull, old, fade, offs, offs2, offs3):
    idx = unstriped8(offs)
    idx2 = unstriped8(offs2)
    idx3 = unstriped8(offs3)
    keysu = unpack_weight(keys_words, keys_scales, "e2m1")
    queryq = mxq(f64(query), 0, "e4m3")
    a = queryq.T @ keysu
    query2q = mxq(f64(query2), 0, "e4m3")
    b = query2q.T @ keysu
    e1s = np.exp(pick8(a, idx, 16))
    s = e1s / (e1s + np.exp(pick8(a, idx2, 16)) + np.exp(pick8(b, idx3, 16))) * f64(lam)
    p = np.exp(s - np.max(s, axis=1, keepdims=True))
    r = p / np.sum(p, axis=1, keepdims=True)
    r1 = np.pad(r, ((0, 0), (1, 0)))[:, :I]
    w = r - r1 * f64(pull)
    ws = w * 256.0
    wf = np.zeros((Q, T))
    wf[np.arange(Q)[:, None], idx[np.arange(Q) % 128 // 16]] = ws
    y = f64(old) * f64(fade) + wf
    return y

@@ -1,0 +1,209 @@
+from contextlib import ExitStack
+
+import concourse.mybir as mybir
+
+D, T, SLOTS, Q = 512, 1024, 512, 128
+FLOPS = 2 * 2 * D * T * Q
+
+F32 = mybir.dt.float32
+BF16 = mybir.dt.bfloat16
+I32 = mybir.dt.int32
+U32 = mybir.dt.uint32
+U16 = mybir.dt.uint16
+U8 = mybir.dt.uint8
+FP8X4 = mybir.dt.float8_e4m3fn_x4
+FP4X4 = mybir.dt.float4_e2m1fn_x4
+ALU = mybir.AluOpType
+ACT = mybir.ActivationFunctionType
+
+P = 128
+PACK = 4
+BANK = 512
+HALF = SLOTS // 2
+LIST_COLS = HALF // 16
+CAP = 2.0 ** 31
+
+
+def tile_attend_quotaratio_stepwise_counts_heads_kernel(
+    tc, query, query2, keys_words, keys_scales, lam, pull, old, fade, offs, offs2, offs3, out
+):
+    nc = tc.nc
+    with ExitStack() as ctx:
+        keep = ctx.enter_context(tc.tile_pool(name="keep", bufs=1))
+        psum = ctx.enter_context(tc.psum_pool(name="psum", bufs=1))
+
+        list1 = keep.tile([P, SLOTS // 16], U16, name="list1")
+        list2 = keep.tile([P, SLOTS // 16], U16, name="list2")
+        list3 = keep.tile([P, SLOTS // 16], U16, name="list3")
+
+        key_scales = keep.tile([P, T], U8, name="key_scales", align_bytes=64)
+        nc.gpsimd.memset(key_scales[:].bitcast(I32), 0)
+        before = keep.tile([P, SLOTS], F32, name="before")
+        zero = keep.tile([P, 1], F32, name="zero")
+        nc.vector.memset(zero[:], 0.0)
+
+        placed = keep.tile([P, T], F32, name="placed")
+        nc.vector.memset(placed[:], 0.0)
+        raw1 = keep.tile([P, PACK, Q], F32, name="raw1")
+        raw2 = keep.tile([P, PACK, Q], F32, name="raw2")
+        key_words = keep.tile([P, 2 * T], U8, name="key_words", align_bytes=64)
+        nc.sync.dma_start(out=raw1[:], in_=query.rearrange("(p j) q -> p j q", j=PACK))
+        nc.sync.dma_start(out=key_words[:].bitcast(I32), in_=keys_words[0].bitcast(I32))
+        for quad in range(4):
+            nc.scalar.dma_start(
+                out=key_scales[32 * quad : 32 * quad + 4, :].bitcast(I32),
+                in_=keys_scales[0, 4 * quad : 4 * quad + 4, :].bitcast(I32),
+            )
+        nc.scalar.activation(before[:, 0:1], zero[:], ACT.Copy)
+        nc.sync.dma_start(out=raw2[:], in_=query2.rearrange("(p j) q -> p j q", j=PACK))
+        nc.sync.dma_start(list1[:], offs)
+        nc.sync.dma_start(list2[:], offs2)
+        nc.sync.dma_start(list3[:], offs3)
+        lam_t = keep.tile([P, 1], F32, name="lam_t")
+        pull_t = keep.tile([P, 1], F32, name="pull_t")
+        fade_t = keep.tile([P, 1], F32, name="fade_t")
+        old_t = keep.tile([P, T], F32, name="old_t")
+        nc.gpsimd.dma_start(out=lam_t[:], in_=lam)
+        nc.gpsimd.dma_start(out=pull_t[:], in_=pull)
+        nc.gpsimd.dma_start(out=fade_t[:], in_=fade)
+        nc.sync.dma_start(out=old_t[:], in_=old)
+
+        inv_lam = keep.tile([P, 1], F32, name="inv_lam")
+        neg_inv_lam = keep.tile([P, 1], F32, name="neg_inv_lam")
+        neg_pull = keep.tile([P, 1], F32, name="neg_pull")
+        nc.gpsimd.tensor_scalar(neg_pull[:], pull_t[:], -1.0, 1.0, ALU.mult, ALU.mult)
+
+        grouped1 = keep.tile([P, Q, PACK], BF16, name="grouped1", align_bytes=64)
+        grouped2 = keep.tile([P, Q, PACK], BF16, name="grouped2", align_bytes=64)
+        codes1 = keep.tile([P, Q], U32, name="codes1", align_bytes=64)
+        codes2 = keep.tile([P, Q], U32, name="codes2", align_bytes=64)
+        scales1 = keep.tile([P, Q], U8, name="scales1", align_bytes=64)
+        scales2 = keep.tile([P, Q], U8, name="scales2", align_bytes=64)
+        nc.vector.tensor_copy(out=grouped1[:], in_=raw1[:].rearrange("p j q -> p q j"))
+        nc.vector.quantize_mx(out=codes1[:].bitcast(FP8X4), scales=scales1[:], in_=grouped1[:].rearrange("p q j -> p (q j)"))
+        nc.vector.tensor_copy(out=grouped2[:], in_=raw2[:].rearrange("p j q -> p q j"))
+        nc.vector.quantize_mx(out=codes2[:].bitcast(FP8X4), scales=scales2[:], in_=grouped2[:].rearrange("p q j -> p (q j)"))
+
+        a_sb = keep.tile([P, T], F32, name="a_sb")
+        b_sb = keep.tile([P, T], F32, name="b_sb")
+
+        def score(name, codes, scales, lo, hi):
+            bank = psum.tile([P, hi - lo], F32, name="%s_bank%d" % (name, lo))
+            nc.tensor.matmul_mx(
+                out=bank[:],
+                lhsT=codes[:].bitcast(FP8X4),
+                lhsT_scale=scales[:],
+                rhs=key_words[:, 2 * lo : 2 * hi].bitcast(FP4X4),
+                rhs_scale=key_scales[:, lo:hi],
+                start=True,
+                stop=True,
+            )
+            return bank
+
+        for lo in range(0, T, 256):
+            bank = score("a", codes1, scales1, lo, lo + 256)
+            if lo + 256 < T:
+                nc.scalar.copy(out=a_sb[:, lo : lo + 256], in_=bank[:])
+            else:
+                nc.vector.tensor_copy(out=a_sb[:, lo : lo + 256], in_=bank[:])
+        for lo, hi in ((0, 512), (512, 768), (768, 1024)):
+            bank = score("b", codes2, scales2, lo, hi)
+            nc.vector.tensor_copy(out=b_sb[:, lo:hi], in_=bank[:])
+
+        def t32(name, width, tag=None):
+            return keep.tile([P, width], F32, name=name, tag=tag or name)
+
+        e1n = [t32("e1n0", HALF), None]
+        e2 = [t32("e2_%d" % h, HALF) for h in range(2)]
+        e3 = [t32("e3_%d" % h, HALF) for h in range(2)]
+        b3 = [t32("b3_%d" % h, HALF) for h in range(2)]
+        cols = [slice(h * LIST_COLS, (h + 1) * LIST_COLS) for h in range(2)]
+        nc.scalar.activation(e1n[0][:], a_sb[:].indirect(list1[:, cols[0]]), ACT.Exp, scale=-1.0)
+        nc.scalar.activation(e2[0][:], a_sb[:].indirect(list2[:, cols[0]]), ACT.Exp)
+        nc.scalar.activation(e2[1][:], a_sb[:].indirect(list2[:, cols[1]]), ACT.Exp)
+        for h in range(2):
+            nc.vector.tensor_copy(b3[h][:], b_sb[:].indirect(list3[:, cols[h]]))
+        nc.vector.reciprocal(inv_lam[:], lam_t[:])
+        nc.vector.tensor_scalar(neg_inv_lam[:], inv_lam[:], -1.0, None, ALU.mult)
+        nc.scalar.activation(e3[0][:], b3[0][:], ACT.Exp)
+        nc.scalar.activation(e3[1][:], b3[1][:], ACT.Exp)
+        e1n[1] = t32("e1n1", HALF, tag="b3_0")
+        nc.scalar.activation(e1n[1][:], a_sb[:].indirect(list1[:, cols[1]]), ACT.Exp, scale=-1.0)
+
+        faded = keep.tile([P, T], F32, name="faded", tag="b3_1")
+        nc.scalar.activation(faded[:], old_t[:], ACT.Copy, scale=fade_t[:])
+
+        n2, n4 = HALF // 2, HALF // 4
+        rest = [t32("rest%d" % h, HALF) for h in range(2)]
+        odds = [t32("odds%d" % h, HALF) for h in range(2)]
+        den = [t32("den%d" % h, HALF) for h in range(2)]
+        scaled = [t32("scaled%d" % h, HALF) for h in range(2)]
+        top = [t32("top%d" % h, 1) for h in range(2)]
+        inv = [t32("inv%d" % h, HALF) for h in range(2)]
+        pairs = [t32("pairs%d" % h, n2) for h in range(2)]
+        inv2 = [t32("inv2_%d" % h, n2) for h in range(2)]
+        fours = [t32("fours%d" % h, n4) for h in range(2)]
+        inv4 = [t32("inv4_%d" % h, n4) for h in range(2)]
+        neg_top = t32("neg_top", 1)
+        tt = nc.vector.tensor_tensor
+
+        def step_mx(h):
+            start = top[h - 1][:] if h else None
+            nc.vector.tensor_scalar(scaled[h][:], den[h][:], neg_inv_lam[:], start, ALU.mult, ALU.max, accum_out=top[h][:])
+
+        def up1(h):
+            tt(pairs[h][:], den[h][:, 0:n2], den[h][:, n2:HALF], ALU.mult)
+
+        def up2(h):
+            tt(fours[h][:], pairs[h][:, 0:n4], pairs[h][:, n4:n2], ALU.mult)
+
+        def down1(h):
+            tt(inv2[h][:, 0:n4], inv4[h][:], pairs[h][:, n4:n2], ALU.mult)
+            tt(inv2[h][:, n4:n2], inv4[h][:], pairs[h][:, 0:n4], ALU.mult)
+
+        def down2(h):
+            tt(inv[h][:, 0:n2], inv2[h][:], den[h][:, n2:HALF], ALU.mult)
+            tt(inv[h][:, n2:HALF], inv2[h][:], den[h][:, 0:n2], ALU.mult)
+
+        for h in range(2):
+            tt(rest[h][:], e2[h][:], e3[h][:], ALU.add)
+        for h in range(2):
+            tt(odds[h][:], rest[h][:], e1n[h][:], ALU.mult)
+        for h in range(2):
+            nc.vector.tensor_scalar(den[h][:], odds[h][:], 1.0, CAP, ALU.add, ALU.min)
+        up1(0)
+        step_mx(0)
+        up2(0)
+        step_mx(1)
+        nc.vector.reciprocal(inv4[0][:], fours[0][:])
+        nc.vector.reciprocal(neg_top[:], top[1][:])
+        up1(1)
+        down1(0)
+        up2(1)
+        down2(0)
+        nc.vector.reciprocal(inv4[1][:], fours[1][:])
+        down1(1)
+        down2(1)
+
+        p = t32("p", SLOTS)
+        sums = []
+        for h in range(2):
+            lo, hi = h * HALF, (h + 1) * HALF
+            sums.append(t32("sum%d" % h, 1))
+            nc.scalar.activation(p[:, lo:hi], inv[h][:], ACT.Exp, bias=neg_top[:], scale=lam_t[:], accum_out=sums[h][:])
+            last = min(hi, SLOTS - 1)
+            nc.scalar.activation(before[:, lo + 1 : last + 1], p[:, lo:last], ACT.Copy, scale=neg_pull[:])
+            if h == 1:
+                both = t32("both", 1)
+                total = t32("total", 1)
+                gain = t32("gain", 1)
+                nc.scalar.activation(both[:], sums[0][:], ACT.Identity, bias=sums[1][:])
+                nc.scalar.activation(total[:], both[:], ACT.Copy, scale=1.0 / 256.0)
+                nc.vector.reciprocal(gain[:], total[:])
+            nc.vector.tensor_tensor(placed[:].indirect(list1[:, cols[h]]), p[:, lo:hi], before[:, lo:hi], ALU.add)
+
+        for part, queue in enumerate((nc.sync, nc.scalar, nc.sync, nc.scalar)):
+            piece = slice(part * 256, (part + 1) * 256)
+            res = t32("res%d" % part, 256)
+            nc.vector.scalar_tensor_tensor(res[:], placed[:, piece], gain[:], faded[:, piece], ALU.mult, ALU.add)
+            queue.dma_start(out=out[:, piece], in_=res[:])

@@ -37,13 +37,13 @@ def tile_attend_quotaratio_stepwise_counts_heads_kernel(
         list3 = keep.tile([P, SLOTS // 16], U16, name="list3")
 
         key_scales = keep.tile([P, T], U8, name="key_scales", align_bytes=64)
-        nc.gpsimd.memset(key_scales[:].bitcast(I32), 0)
+        nc.vector.memset(key_scales[:].bitcast(I32), 0)
+        placed = keep.tile([P, T], F32, name="placed")
+        nc.vector.memset(placed[:], 0.0)
         before = keep.tile([P, SLOTS], F32, name="before")
         zero = keep.tile([P, 1], F32, name="zero")
         nc.vector.memset(zero[:], 0.0)
 
-        placed = keep.tile([P, T], F32, name="placed")
-        nc.vector.memset(placed[:], 0.0)
         raw1 = keep.tile([P, PACK, Q], F32, name="raw1")
         raw2 = keep.tile([P, PACK, Q], F32, name="raw2")
         key_words = keep.tile([P, 2 * T], U8, name="key_words", align_bytes=64)
@@ -63,15 +63,16 @@ def tile_attend_quotaratio_stepwise_counts_heads_kernel(
         pull_t = keep.tile([P, 1], F32, name="pull_t")
         fade_t = keep.tile([P, 1], F32, name="fade_t")
         old_t = keep.tile([P, T], F32, name="old_t")
-        nc.gpsimd.dma_start(out=lam_t[:], in_=lam)
-        nc.gpsimd.dma_start(out=pull_t[:], in_=pull)
-        nc.gpsimd.dma_start(out=fade_t[:], in_=fade)
+        nc.sync.dma_start(out=lam_t[:], in_=lam)
+        nc.sync.dma_start(out=pull_t[:], in_=pull)
+        nc.sync.dma_start(out=fade_t[:], in_=fade)
         nc.sync.dma_start(out=old_t[:], in_=old)
 
         inv_lam = keep.tile([P, 1], F32, name="inv_lam")
         neg_inv_lam = keep.tile([P, 1], F32, name="neg_inv_lam")
-        neg_pull = keep.tile([P, 1], F32, name="neg_pull")
-        nc.gpsimd.tensor_scalar(neg_pull[:], pull_t[:], -1.0, 1.0, ALU.mult, ALU.mult)
+        neg_pull = [keep.tile([P, 1], F32, name="neg_pull%d" % h) for h in range(2)]
+        for h in range(2):
+            nc.gpsimd.tensor_scalar(neg_pull[h][:], pull_t[:], -1.0, 1.0, ALU.mult, ALU.mult)
 
         grouped1 = keep.tile([P, Q, PACK], BF16, name="grouped1", align_bytes=64)
         grouped2 = keep.tile([P, Q, PACK], BF16, name="grouped2", align_bytes=64)
@@ -116,25 +117,24 @@ def tile_attend_quotaratio_stepwise_counts_heads_kernel(
         e1n = [t32("e1n0", HALF), None]
         e2 = [t32("e2_%d" % h, HALF) for h in range(2)]
         e3 = [t32("e3_%d" % h, HALF) for h in range(2)]
-        b3 = [t32("b3_%d" % h, HALF) for h in range(2)]
+        a2_late = t32("a2_late", HALF)
         cols = [slice(h * LIST_COLS, (h + 1) * LIST_COLS) for h in range(2)]
-        nc.scalar.activation(e1n[0][:], a_sb[:].indirect(list1[:, cols[0]]), ACT.Exp, scale=-1.0)
-        nc.scalar.activation(e2[0][:], a_sb[:].indirect(list2[:, cols[0]]), ACT.Exp)
-        nc.scalar.activation(e2[1][:], a_sb[:].indirect(list2[:, cols[1]]), ACT.Exp)
-        for h in range(2):
-            nc.vector.tensor_copy(b3[h][:], b_sb[:].indirect(list3[:, cols[h]]))
+        nc.vector.tensor_copy(a2_late[:], a_sb[:].indirect(list2[:, cols[1]]))
         nc.vector.reciprocal(inv_lam[:], lam_t[:])
         nc.vector.tensor_scalar(neg_inv_lam[:], inv_lam[:], -1.0, None, ALU.mult)
-        nc.scalar.activation(e3[0][:], b3[0][:], ACT.Exp)
-        nc.scalar.activation(e3[1][:], b3[1][:], ACT.Exp)
-        e1n[1] = t32("e1n1", HALF, tag="b3_0")
+        nc.scalar.activation(e1n[0][:], a_sb[:].indirect(list1[:, cols[0]]), ACT.Exp, scale=-1.0)
+        nc.scalar.activation(e2[0][:], a_sb[:].indirect(list2[:, cols[0]]), ACT.Exp)
+        nc.scalar.activation(e3[0][:], b_sb[:].indirect(list3[:, cols[0]]), ACT.Exp)
+        nc.scalar.activation(e3[1][:], b_sb[:].indirect(list3[:, cols[1]]), ACT.Exp)
+        nc.scalar.activation(e2[1][:], a2_late[:], ACT.Exp)
+        e1n[1] = t32("e1n1", HALF, tag="b_sb")
         nc.scalar.activation(e1n[1][:], a_sb[:].indirect(list1[:, cols[1]]), ACT.Exp, scale=-1.0)
 
-        faded = keep.tile([P, T], F32, name="faded", tag="b3_1")
+        faded = keep.tile([P, T], F32, name="faded", tag="a_sb")
         nc.scalar.activation(faded[:], old_t[:], ACT.Copy, scale=fade_t[:])
 
         n2, n4 = HALF // 2, HALF // 4
-        rest = [t32("rest%d" % h, HALF) for h in range(2)]
+        rest = [t32("rest0", HALF), None]
         odds = [t32("odds%d" % h, HALF) for h in range(2)]
         den = [t32("den%d" % h, HALF) for h in range(2)]
         scaled = [t32("scaled%d" % h, HALF) for h in range(2)]
@@ -165,42 +165,52 @@ def tile_attend_quotaratio_stepwise_counts_heads_kernel(
             tt(inv[h][:, 0:n2], inv2[h][:], den[h][:, n2:HALF], ALU.mult)
             tt(inv[h][:, n2:HALF], inv2[h][:], den[h][:, 0:n2], ALU.mult)
 
-        for h in range(2):
+        def step_t(h):
             tt(rest[h][:], e2[h][:], e3[h][:], ALU.add)
-        for h in range(2):
+
+        def step_y(h):
             tt(odds[h][:], rest[h][:], e1n[h][:], ALU.mult)
-        for h in range(2):
+
+        def step_c(h):
             nc.vector.tensor_scalar(den[h][:], odds[h][:], 1.0, CAP, ALU.add, ALU.min)
+
+        step_t(0)
+        step_y(0)
+        step_c(0)
         up1(0)
         step_mx(0)
         up2(0)
-        step_mx(1)
+        rest[1] = t32("rest1", HALF, tag="odds0")
+        step_t(1)
         nc.vector.reciprocal(inv4[0][:], fours[0][:])
-        nc.vector.reciprocal(neg_top[:], top[1][:])
-        up1(1)
+        step_y(1)
         down1(0)
-        up2(1)
+        step_c(1)
         down2(0)
+        step_mx(1)
+        up1(1)
+        nc.vector.reciprocal(neg_top[:], top[1][:])
+        up2(1)
         nc.vector.reciprocal(inv4[1][:], fours[1][:])
         down1(1)
         down2(1)
 
-        p = t32("p", SLOTS)
+        p = [t32("p%d" % h, HALF) for h in range(2)]
         sums = []
         for h in range(2):
             lo, hi = h * HALF, (h + 1) * HALF
-            sums.append(t32("sum%d" % h, 1))
-            nc.scalar.activation(p[:, lo:hi], inv[h][:], ACT.Exp, bias=neg_top[:], scale=lam_t[:], accum_out=sums[h][:])
+            sums.append(t32("sum%d" % h, 1, tag="neg_pull0" if h else None))
+            nc.scalar.activation(p[h][:], inv[h][:], ACT.Exp, bias=neg_top[:], scale=lam_t[:], accum_out=sums[h][:])
             last = min(hi, SLOTS - 1)
-            nc.scalar.activation(before[:, lo + 1 : last + 1], p[:, lo:last], ACT.Copy, scale=neg_pull[:])
+            nc.scalar.activation(before[:, lo + 1 : last + 1], p[h][:, 0 : last - lo], ACT.Copy, scale=neg_pull[h][:])
             if h == 1:
                 both = t32("both", 1)
                 total = t32("total", 1)
-                gain = t32("gain", 1)
+                gain = t32("gain", 1, tag="p0")
                 nc.scalar.activation(both[:], sums[0][:], ACT.Identity, bias=sums[1][:])
                 nc.scalar.activation(total[:], both[:], ACT.Copy, scale=1.0 / 256.0)
                 nc.vector.reciprocal(gain[:], total[:])
-            nc.vector.tensor_tensor(placed[:].indirect(list1[:, cols[h]]), p[:, lo:hi], before[:, lo:hi], ALU.add)
+            nc.vector.tensor_tensor(placed[:].indirect(list1[:, cols[h]]), p[h][:], before[:, lo:hi], ALU.add)
 
         for part, queue in enumerate((nc.sync, nc.scalar, nc.sync, nc.scalar)):
             piece = slice(part * 256, (part + 1) * 256)

@@ -151,49 +151,58 @@ def tile_attend_quotaratio_stepwise_counts_heads_kernel(
             start = top[h - 1][:] if h else None
             nc.vector.tensor_scalar(scaled[h][:], den[h][:], neg_inv_lam[:], start, ALU.mult, ALU.max, accum_out=top[h][:])
 
-        def up1(h):
-            tt(pairs[h][:], den[h][:, 0:n2], den[h][:, n2:HALF], ALU.mult)
+        both_groups, groups = slice(0, 2), (slice(0, 1), slice(1, 2))
 
-        def up2(h):
-            tt(fours[h][:], pairs[h][:, 0:n4], pairs[h][:, n4:n2], ALU.mult)
+        def split(tile, g):
+            return tile[:].rearrange("p (g j c) -> p g j c", g=2, j=2)[:, g]
 
-        def down1(h):
-            tt(inv2[h][:, 0:n4], inv4[h][:], pairs[h][:, n4:n2], ALU.mult)
-            tt(inv2[h][:, n4:n2], inv4[h][:], pairs[h][:, 0:n4], ALU.mult)
+        def twice(tile, g):
+            view = tile[:].rearrange("p (g c) -> p g c", g=2)[:, g]
+            return view.unsqueeze(2).to_broadcast([P, view.shape[1], 2, view.shape[2]])
 
-        def down2(h):
-            tt(inv[h][:, 0:n2], inv2[h][:], den[h][:, n2:HALF], ALU.mult)
-            tt(inv[h][:, n2:HALF], inv2[h][:], den[h][:, 0:n2], ALU.mult)
+        def run(tile, g):
+            width = tile.shape[1] // 2
+            return tile[:, g.start * width : g.stop * width]
 
-        def step_t(h):
-            tt(rest[h][:], e2[h][:], e3[h][:], ALU.add)
+        def join(dst, src):
+            view = split(src, both_groups)
+            tt(dst[:].rearrange("p (g c) -> p g c", g=2), view[:, :, 0, :], view[:, :, 1, :], ALU.mult)
 
-        def step_y(h):
-            tt(odds[h][:], rest[h][:], e1n[h][:], ALU.mult)
+        def part(dst, src, inverse, g):
+            tt(split(dst, g), split(src, g)[:, :, ::-1, :], twice(inverse, g), ALU.mult)
 
-        def step_c(h):
-            nc.vector.tensor_scalar(den[h][:], odds[h][:], 1.0, CAP, ALU.add, ALU.min)
+        def step_t(h, g):
+            tt(run(rest[h], g), run(e2[h], g), run(e3[h], g), ALU.add)
 
-        step_t(0)
-        step_y(0)
-        step_c(0)
-        up1(0)
+        def step_y(h, g):
+            tt(run(odds[h], g), run(rest[h], g), run(e1n[h], g), ALU.mult)
+
+        def step_c(h, g):
+            nc.vector.tensor_scalar(run(den[h], g), run(odds[h], g), 1.0, CAP, ALU.add, ALU.min)
+
+        for step in (step_t, step_y, step_c):
+            for g in groups:
+                step(0, g)
+        rest[1] = t32("rest1", HALF, tag="rest0")
+        step_t(1, both_groups)
+        join(pairs[0], den[0])
         step_mx(0)
-        up2(0)
-        rest[1] = t32("rest1", HALF, tag="odds0")
-        step_t(1)
+        join(fours[0], pairs[0])
+        step_y(1, both_groups)
         nc.vector.reciprocal(inv4[0][:], fours[0][:])
-        step_y(1)
-        down1(0)
-        step_c(1)
-        down2(0)
+        step_c(1, both_groups)
+        part(inv2[0], pairs[0], inv4[0], both_groups)
+        join(pairs[1], den[1])
         step_mx(1)
-        up1(1)
+        join(fours[1], pairs[1])
+        part(inv[0], den[0], inv2[0], both_groups)
         nc.vector.reciprocal(neg_top[:], top[1][:])
-        up2(1)
-        nc.vector.reciprocal(inv4[1][:], fours[1][:])
-        down1(1)
-        down2(1)
+        for g in groups:
+            nc.vector.reciprocal(run(inv4[1], g), run(fours[1], g))
+        for g in groups:
+            part(inv2[1], pairs[1], inv4[1], g)
+        for g in groups:
+            part(inv[1], den[1], inv2[1], g)
 
         p = [t32("p%d" % h, HALF) for h in range(2)]
         sums = []

from contextlib import ExitStack

import concourse.mybir as mybir

D, T, SLOTS, Q = 512, 1024, 512, 128
FLOPS = 2 * 2 * D * T * Q

F32 = mybir.dt.float32
BF16 = mybir.dt.bfloat16
I32 = mybir.dt.int32
U32 = mybir.dt.uint32
U16 = mybir.dt.uint16
U8 = mybir.dt.uint8
FP8X4 = mybir.dt.float8_e4m3fn_x4
FP4X4 = mybir.dt.float4_e2m1fn_x4
ALU = mybir.AluOpType
ACT = mybir.ActivationFunctionType

P = 128
PACK = 4
BANK = 512
HALF = SLOTS // 2
LIST_COLS = HALF // 16
CAP = 2.0 ** 31


def tile_attend_quotaratio_stepwise_counts_heads_kernel(
    tc, query, query2, keys_words, keys_scales, lam, pull, old, fade, offs, offs2, offs3, out
):
    nc = tc.nc
    with ExitStack() as ctx:
        keep = ctx.enter_context(tc.tile_pool(name="keep", bufs=1))
        psum = ctx.enter_context(tc.psum_pool(name="psum", bufs=1))

        list1 = keep.tile([P, SLOTS // 16], U16, name="list1")
        list2 = keep.tile([P, SLOTS // 16], U16, name="list2")
        list3 = keep.tile([P, SLOTS // 16], U16, name="list3")

        key_scales = keep.tile([P, T], U8, name="key_scales", align_bytes=64)
        nc.vector.memset(key_scales[:].bitcast(I32), 0)
        placed = keep.tile([P, T], F32, name="placed")
        nc.vector.memset(placed[:], 0.0)
        before = keep.tile([P, SLOTS], F32, name="before")
        zero = keep.tile([P, 1], F32, name="zero")
        nc.vector.memset(zero[:], 0.0)

        raw1 = keep.tile([P, PACK, Q], F32, name="raw1")
        raw2 = keep.tile([P, PACK, Q], F32, name="raw2")
        key_words = keep.tile([P, 2 * T], U8, name="key_words", align_bytes=64)
        nc.sync.dma_start(out=raw1[:], in_=query.rearrange("(p j) q -> p j q", j=PACK))
        nc.sync.dma_start(out=key_words[:].bitcast(I32), in_=keys_words[0].bitcast(I32))
        for quad in range(4):
            nc.scalar.dma_start(
                out=key_scales[32 * quad : 32 * quad + 4, :].bitcast(I32),
                in_=keys_scales[0, 4 * quad : 4 * quad + 4, :].bitcast(I32),
            )
        nc.scalar.activation(before[:, 0:1], zero[:], ACT.Copy)
        nc.sync.dma_start(out=raw2[:], in_=query2.rearrange("(p j) q -> p j q", j=PACK))
        nc.sync.dma_start(list1[:], offs)
        nc.sync.dma_start(list2[:], offs2)
        nc.sync.dma_start(list3[:], offs3)
        lam_t = keep.tile([P, 1], F32, name="lam_t")
        pull_t = keep.tile([P, 1], F32, name="pull_t")
        fade_t = keep.tile([P, 1], F32, name="fade_t")
        old_t = keep.tile([P, T], F32, name="old_t")
        nc.sync.dma_start(out=lam_t[:], in_=lam)
        nc.sync.dma_start(out=pull_t[:], in_=pull)
        nc.sync.dma_start(out=fade_t[:], in_=fade)
        nc.sync.dma_start(out=old_t[:], in_=old)

        inv_lam = keep.tile([P, 1], F32, name="inv_lam")
        neg_inv_lam = keep.tile([P, 1], F32, name="neg_inv_lam")
        neg_pull = [keep.tile([P, 1], F32, name="neg_pull%d" % h) for h in range(2)]
        for h in range(2):
            nc.gpsimd.tensor_scalar(neg_pull[h][:], pull_t[:], -1.0, 1.0, ALU.mult, ALU.mult)

        grouped1 = keep.tile([P, Q, PACK], BF16, name="grouped1", align_bytes=64)
        grouped2 = keep.tile([P, Q, PACK], BF16, name="grouped2", align_bytes=64)
        codes1 = keep.tile([P, Q], U32, name="codes1", align_bytes=64)
        codes2 = keep.tile([P, Q], U32, name="codes2", align_bytes=64)
        scales1 = keep.tile([P, Q], U8, name="scales1", align_bytes=64)
        scales2 = keep.tile([P, Q], U8, name="scales2", align_bytes=64)
        nc.vector.tensor_copy(out=grouped1[:], in_=raw1[:].rearrange("p j q -> p q j"))
        nc.vector.quantize_mx(out=codes1[:].bitcast(FP8X4), scales=scales1[:], in_=grouped1[:].rearrange("p q j -> p (q j)"))
        nc.vector.tensor_copy(out=grouped2[:], in_=raw2[:].rearrange("p j q -> p q j"))
        nc.vector.quantize_mx(out=codes2[:].bitcast(FP8X4), scales=scales2[:], in_=grouped2[:].rearrange("p q j -> p (q j)"))

        a_sb = keep.tile([P, T], F32, name="a_sb")
        b_sb = keep.tile([P, T], F32, name="b_sb")

        def score(name, codes, scales, lo, hi):
            bank = psum.tile([P, hi - lo], F32, name="%s_bank%d" % (name, lo))
            nc.tensor.matmul_mx(
                out=bank[:],
                lhsT=codes[:].bitcast(FP8X4),
                lhsT_scale=scales[:],
                rhs=key_words[:, 2 * lo : 2 * hi].bitcast(FP4X4),
                rhs_scale=key_scales[:, lo:hi],
                start=True,
                stop=True,
            )
            return bank

        for lo in range(0, T, 256):
            bank = score("a", codes1, scales1, lo, lo + 256)
            if lo + 256 < T:
                nc.scalar.copy(out=a_sb[:, lo : lo + 256], in_=bank[:])
            else:
                nc.vector.tensor_copy(out=a_sb[:, lo : lo + 256], in_=bank[:])
        for lo, hi in ((0, 512), (512, 768), (768, 1024)):
            bank = score("b", codes2, scales2, lo, hi)
            nc.vector.tensor_copy(out=b_sb[:, lo:hi], in_=bank[:])

        def t32(name, width, tag=None):
            return keep.tile([P, width], F32, name=name, tag=tag or name)

        e1n = [t32("e1n0", HALF), None]
        e2 = [t32("e2_%d" % h, HALF) for h in range(2)]
        e3 = [t32("e3_%d" % h, HALF) for h in range(2)]
        a2_late = t32("a2_late", HALF)
        cols = [slice(h * LIST_COLS, (h + 1) * LIST_COLS) for h in range(2)]
        nc.vector.tensor_copy(a2_late[:], a_sb[:].indirect(list2[:, cols[1]]))
        nc.vector.reciprocal(inv_lam[:], lam_t[:])
        nc.vector.tensor_scalar(neg_inv_lam[:], inv_lam[:], -1.0, None, ALU.mult)
        nc.scalar.activation(e1n[0][:], a_sb[:].indirect(list1[:, cols[0]]), ACT.Exp, scale=-1.0)
        nc.scalar.activation(e2[0][:], a_sb[:].indirect(list2[:, cols[0]]), ACT.Exp)
        nc.scalar.activation(e3[0][:], b_sb[:].indirect(list3[:, cols[0]]), ACT.Exp)
        nc.scalar.activation(e3[1][:], b_sb[:].indirect(list3[:, cols[1]]), ACT.Exp)
        nc.scalar.activation(e2[1][:], a2_late[:], ACT.Exp)
        e1n[1] = t32("e1n1", HALF, tag="b_sb")
        nc.scalar.activation(e1n[1][:], a_sb[:].indirect(list1[:, cols[1]]), ACT.Exp, scale=-1.0)

        faded = keep.tile([P, T], F32, name="faded", tag="a_sb")
        nc.scalar.activation(faded[:], old_t[:], ACT.Copy, scale=fade_t[:])

        n2, n4 = HALF // 2, HALF // 4
        rest = [t32("rest0", HALF), None]
        odds = [t32("odds%d" % h, HALF) for h in range(2)]
        den = [t32("den%d" % h, HALF) for h in range(2)]
        scaled = [t32("scaled%d" % h, HALF) for h in range(2)]
        top = [t32("top%d" % h, 1) for h in range(2)]
        inv = [t32("inv%d" % h, HALF) for h in range(2)]
        pairs = [t32("pairs%d" % h, n2) for h in range(2)]
        inv2 = [t32("inv2_%d" % h, n2) for h in range(2)]
        fours = [t32("fours%d" % h, n4) for h in range(2)]
        inv4 = [t32("inv4_%d" % h, n4) for h in range(2)]
        neg_top = t32("neg_top", 1)
        tt = nc.vector.tensor_tensor

        def step_mx(h):
            start = top[h - 1][:] if h else None
            nc.vector.tensor_scalar(scaled[h][:], den[h][:], neg_inv_lam[:], start, ALU.mult, ALU.max, accum_out=top[h][:])

        both_groups, groups = slice(0, 2), (slice(0, 1), slice(1, 2))

        def split(tile, g):
            return tile[:].rearrange("p (g j c) -> p g j c", g=2, j=2)[:, g]

        def twice(tile, g):
            view = tile[:].rearrange("p (g c) -> p g c", g=2)[:, g]
            return view.unsqueeze(2).to_broadcast([P, view.shape[1], 2, view.shape[2]])

        def run(tile, g):
            width = tile.shape[1] // 2
            return tile[:, g.start * width : g.stop * width]

        def join(dst, src):
            view = split(src, both_groups)
            tt(dst[:].rearrange("p (g c) -> p g c", g=2), view[:, :, 0, :], view[:, :, 1, :], ALU.mult)

        def part(dst, src, inverse, g):
            tt(split(dst, g), split(src, g)[:, :, ::-1, :], twice(inverse, g), ALU.mult)

        def step_t(h, g):
            tt(run(rest[h], g), run(e2[h], g), run(e3[h], g), ALU.add)

        def step_y(h, g):
            tt(run(odds[h], g), run(rest[h], g), run(e1n[h], g), ALU.mult)

        def step_c(h, g):
            nc.vector.tensor_scalar(run(den[h], g), run(odds[h], g), 1.0, CAP, ALU.add, ALU.min)

        for step in (step_t, step_y, step_c):
            for g in groups:
                step(0, g)
        rest[1] = t32("rest1", HALF, tag="rest0")
        step_t(1, both_groups)
        join(pairs[0], den[0])
        step_mx(0)
        join(fours[0], pairs[0])
        step_y(1, both_groups)
        nc.vector.reciprocal(inv4[0][:], fours[0][:])
        step_c(1, both_groups)
        part(inv2[0], pairs[0], inv4[0], both_groups)
        join(pairs[1], den[1])
        step_mx(1)
        join(fours[1], pairs[1])
        part(inv[0], den[0], inv2[0], both_groups)
        nc.vector.reciprocal(neg_top[:], top[1][:])
        for g in groups:
            nc.vector.reciprocal(run(inv4[1], g), run(fours[1], g))
        for g in groups:
            part(inv2[1], pairs[1], inv4[1], g)
        for g in groups:
            part(inv[1], den[1], inv2[1], g)

        p = [t32("p%d" % h, HALF) for h in range(2)]
        sums = []
        for h in range(2):
            lo, hi = h * HALF, (h + 1) * HALF
            sums.append(t32("sum%d" % h, 1, tag="neg_pull0" if h else None))
            nc.scalar.activation(p[h][:], inv[h][:], ACT.Exp, bias=neg_top[:], scale=lam_t[:], accum_out=sums[h][:])
            last = min(hi, SLOTS - 1)
            nc.scalar.activation(before[:, lo + 1 : last + 1], p[h][:, 0 : last - lo], ACT.Copy, scale=neg_pull[h][:])
            if h == 1:
                both = t32("both", 1)
                total = t32("total", 1)
                gain = t32("gain", 1, tag="p0")
                nc.scalar.activation(both[:], sums[0][:], ACT.Identity, bias=sums[1][:])
                nc.scalar.activation(total[:], both[:], ACT.Copy, scale=1.0 / 256.0)
                nc.vector.reciprocal(gain[:], total[:])
            nc.vector.tensor_tensor(placed[:].indirect(list1[:, cols[h]]), p[h][:], before[:, lo:hi], ALU.add)

        for part, queue in enumerate((nc.sync, nc.scalar, nc.sync, nc.scalar)):
            piece = slice(part * 256, (part + 1) * 256)
            res = t32("res%d" % part, 256)
            nc.vector.scalar_tensor_tensor(res[:], placed[:, piece], gain[:], faded[:, piece], ALU.mult, ALU.add)
            queue.dma_start(out=out[:, piece], in_=res[:])
